import numpy as np
import ml_dtypes


def mxq(x, axis, fmt="e4m3"):
    dtype, down = {"e4m3": (ml_dtypes.float8_e4m3fn, 7), "e5m2": (ml_dtypes.float8_e5m2, 14)}[fmt]
    v = np.moveaxis(np.asarray(x, np.float32).astype(ml_dtypes.bfloat16).astype(np.float64), axis, -1)
    blocks = v.reshape(v.shape[:-1] + (-1, 32))
    amax = np.abs(blocks).max(-1, keepdims=True)
    byte = np.maximum(np.where(amax > 0, np.frexp(amax)[1] - 1 + 127, 0) - down, 1)
    scale = np.exp2(byte - 127.0)
    codes = (blocks / scale).astype(np.float32).astype(dtype).astype(np.float64)
    return np.moveaxis((codes * scale).reshape(v.shape), -1, axis)


WIDE = False


def mx_kscale(k):
    if not WIDE:
        return np.ones(k)
    levels = np.array([10, -10, 5, -5, 0])
    if k % 512:
        return np.exp2(np.random.permutation(np.resize(levels, k // 32))).repeat(32)
    a = np.empty((k // 512, 16))
    for p in range(k // 512):
        a[p, :8] = np.random.permutation(np.resize(levels, 8))
        for g in range(8):
            far = levels[np.abs(levels - a[p, g]) >= 10]
            a[p, g + 8] = far[np.random.randint(len(far))]
    return np.exp2(a.ravel()).repeat(32)


def f64(x):
    return np.asarray(x).astype(np.float64)


def striped(idx):
    return np.tile(idx.reshape(-1, 16).T, (8, 1)).astype(np.uint16)


def unstriped(offs):
    return offs[:16].T.reshape(-1).astype(np.int64)


def striped8(idx):
    return np.concatenate([x.reshape(-1, 16).T for x in idx]).astype(np.uint16)


def runs(offs, k):
    lists = np.stack([offs[16 * r : 16 * r + 16].T.reshape(-1) for r in range(8)]).astype(np.int64)
    return lists[np.arange(k) % 512 // 64]


def pack_weight(w):
    k, n = w.shape
    w = f64(np.asarray(w, np.float32).astype(ml_dtypes.bfloat16)).reshape(k // 32, 32, n)
    amax = np.abs(w).max(1)
    byte = np.clip(np.where(amax > 0, np.frexp(amax)[1] - 1 + 127 - 7, 1), 1, 254)
    scaled = (w * np.exp2(127.0 - byte)[:, None, :]).reshape(k, n).astype(np.float32)
    words = np.ascontiguousarray(scaled.reshape(k // 512, 128, 4, n).transpose(0, 1, 3, 2)).astype(ml_dtypes.float8_e4m3fn).view(np.uint8)
    return words, np.ascontiguousarray(byte.astype(np.uint8).reshape(k // 512, 16, n))


def unpack_weight(words, scales):
    g, p, n, _ = words.shape
    vals = np.ascontiguousarray(words).view(ml_dtypes.float8_e4m3fn).astype(np.float64) * np.repeat(np.exp2(scales.astype(np.float64) - 127.0), 8, axis=1)[..., None]
    return vals.transpose(0, 1, 3, 2).reshape(g * 512, n)


def sigmoid(v):
    return 1.0 / (1.0 + np.exp(-np.maximum(v, -700.0)))


K, T, S, N, H = 512, 2048, 512, 512, 512


def setup_inputs():
    n = np.random.standard_normal
    s = mx_kscale(K)[:, None]
    u = mx_kscale(H)
    packed_xT = pack_weight(n((K, T)) * s)
    return {
        "x_words": packed_xT[0],
        "x_scales": packed_xT[1],
        "w1": (n((K, H)) / np.sqrt(K) / s).astype(np.float32),
        "gn": (np.random.uniform(0.5, 1.5, (H, 1)) * u[:, None]).astype(np.float32),
        "w2": (n((H, N)) / np.sqrt(H) / u[:, None]).astype(np.float32),
        "offs": striped(np.random.permutation(T)[:S]),
        "n1": striped8(np.stack([np.random.permutation(S) for _ in range(8)])),
        "n2": striped8(np.stack([np.random.permutation(S) for _ in range(8)])),
    }


def reference(x_words, x_scales, w1, gn, w2, offs, n1, n2):
    xq = unpack_weight(x_words, x_scales)[:, unstriped(offs)]
    y = sigmoid(mxq(f64(w1), 0, "e4m3").T @ xq)
    lm = 3.5 * (y * (-1.0 * y + 1))
    z = f64(gn) * (0.6 * lm - (0.4 * (lm[np.arange(H)[:, None], runs(n1, H)] + lm[np.arange(H)[:, None], runs(n2, H)])))
    return mxq(f64(w2), 0, "e4m3").T @ mxq(z, 0, "e4m3")

@@ -1,0 +1,206 @@
+from contextlib import ExitStack
+
+import concourse.mybir as mybir
+
+K, T, S, H, N = 512, 2048, 512, 512, 512
+FLOPS = 2 * K * H * S + 2 * H * N * S
+
+F32 = mybir.dt.float32
+BF16 = mybir.dt.bfloat16
+I32 = mybir.dt.int32
+U32 = mybir.dt.uint32
+U16 = mybir.dt.uint16
+U8 = mybir.dt.uint8
+FP8X4 = mybir.dt.float8_e4m3fn_x4
+ACT = mybir.ActivationFunctionType
+ADD = mybir.AluOpType.add
+MULT = mybir.AluOpType.mult
+
+P = 128
+PACK = 4
+HALF = 256
+PIECES = ((0, 256), (256, 128), (384, 128))
+
+
+def tile_picked_cmlmap_none_p_kernel(tc, x_words, x_scales, w1, gn, w2, offs, n1, n2, out):
+    nc = tc.nc
+    with ExitStack() as ctx:
+        keep = ctx.enter_context(tc.tile_pool(name="keep", bufs=1))
+        ring = ctx.enter_context(tc.tile_pool(name="ring", bufs=2))
+        psum = ctx.enter_context(tc.psum_pool(name="psum", bufs=1))
+
+        offs_t = keep.tile([P, S // 16], U16, name="offs_t")
+        n1_t = keep.tile([P, S // 16], U16, name="n1_t")
+        n2_t = keep.tile([P, S // 16], U16, name="n2_t")
+        gn_t = keep.tile([P, PACK], F32, name="gn_t")
+        words_all = keep.tile([P, T], U32, name="words_all", align_bytes=64)
+        scales_all = keep.tile([P, T], U8, name="scales_all", align_bytes=64)
+        w1_raw = [keep.tile([P, PACK, HALF], F32, name="w1_raw", tag=f"raw{h}", align_bytes=64) for h in range(2)]
+        w1_rows = w1.rearrange("(p j) c -> p j c", j=PACK)
+        w2_rows = w2.rearrange("(p j) c -> p j c", j=PACK)
+
+        zero = keep.tile([P, 1], F32, name="zero")
+        zero_bias = keep.tile([P, 1], F32, name="zero_bias")
+        nc.vector.memset(scales_all[:].bitcast(I32), 0)
+        nc.vector.memset(zero[:], 0.0)
+        for q in range(4):
+            nc.scalar.dma_start(
+                scales_all[32 * q : 32 * q + 4, :].bitcast(I32),
+                x_scales[0, 4 * q : 4 * q + 4, :].bitcast(I32),
+            )
+        nc.scalar.activation(zero_bias[:], zero[:], ACT.Tanh)
+
+        nc.sync.dma_start(w1_raw[0][:], w1_rows[:, :, 0:HALF])
+        nc.sync.dma_start(offs_t[:], offs)
+        nc.sync.dma_start(n1_t[:], n1)
+        nc.sync.dma_start(n2_t[:], n2)
+        nc.sync.dma_start(w1_raw[1][:], w1_rows[:, :, HALF:H])
+        nc.sync.dma_start(words_all[:].bitcast(I32), x_words[0].rearrange("p n r -> p (n r)").bitcast(I32))
+        nc.sync.dma_start(gn_t[:], gn.rearrange("(p t) o -> p (t o)", t=PACK))
+
+        w1_bf = keep.tile([P, PACK, P, PACK], BF16, name="w1_bf", align_bytes=64)
+        m_half = HALF // PACK
+        nc.scalar.copy(
+            w1_bf[:, :, 0:m_half, :].rearrange("p t m j -> p m j t"),
+            w1_raw[0][:].rearrange("p j (m t) -> p m j t", t=PACK),
+        )
+        x_scale = keep.tile([P, S], U8, name="x_scale", align_bytes=64)
+        nc.vector.tensor_copy(x_scale[:], scales_all[:].indirect(offs_t[:]))
+        nc.vector.tensor_copy(
+            w1_bf[:, :, m_half:P, :].rearrange("p t m j -> p m j t"),
+            w1_raw[1][:].rearrange("p j (m t) -> p m j t", t=PACK),
+        )
+        w2_raw = [keep.tile([P, PACK, HALF], F32, name="w2_raw", tag=f"raw{h}", align_bytes=64) for h in range(2)]
+        for h in range(2):
+            nc.sync.dma_start(w2_raw[h][:], w2_rows[:, :, h * HALF : (h + 1) * HALF])
+        w1_codes = keep.tile([P, H], U32, name="w1_codes", align_bytes=64)
+        w1_scale = keep.tile([P, H], U8, name="w1_scale", align_bytes=64)
+        nc.vector.quantize_mx(w1_codes[:].bitcast(FP8X4), w1_scale[:], w1_bf[:].rearrange("p t m j -> p (t m j)"))
+
+        gain = keep.tile([P, 3, PACK], F32, name="gain")
+        nc.vector.tensor_scalar(gain[:, 0, :], gn_t[:], 0.35, None, MULT)
+        nc.vector.tensor_scalar(gain[:, 1, :], gn_t[:], -0.525, None, MULT)
+        nc.vector.tensor_scalar(gain[:, 2, :], gn_t[:], 0.525, None, MULT)
+
+        x_codes = keep.tile([P, S], U32, name="x_codes", align_bytes=64)
+        for h in range(2):
+            nc.vector.tensor_copy(
+                x_codes[:, h * HALF : (h + 1) * HALF],
+                words_all[:].indirect(offs_t[:, h * HALF // 16 : (h + 1) * HALF // 16]),
+            )
+
+        w2_bf = keep.tile([P, N, PACK], BF16, name="w2_bf", align_bytes=64)
+
+        def w2_views(h):
+            dst = w2_bf[:, h * HALF : (h + 1) * HALF, :].rearrange("p (c i) t -> p c t i", i=4)
+            src = w2_raw[h][:].rearrange("p t (c i) -> p c t i", i=4)
+            return dst, src
+
+        nc.vector.tensor_copy(*w2_views(0))
+
+        th = keep.tile([P, PACK, S], F32, name="th")
+        sq = keep.tile([P, PACK, S], F32, name="sq")
+        base = keep.tile([P, PACK, S], F32, name="base")
+        window = [keep.tile([P, S], F32, name=f"window{t}", align_bytes=64) for t in range(PACK)]
+        sums = [keep.tile([P, PACK, n], F32, name=f"sums{i}", align_bytes=64) for i, (c, n) in enumerate(PIECES)]
+
+        def first_product(t, c0, n, bank):
+            u = psum.tile([P, S], F32, name="u", tag=bank)
+            nc.tensor.matmul_mx(
+                u[:, 0:n],
+                lhsT=w1_codes[:, t * P : (t + 1) * P].bitcast(FP8X4),
+                lhsT_scale=w1_scale[:, t * P : (t + 1) * P],
+                rhs=x_codes[:, c0 : c0 + n].bitcast(FP8X4),
+                rhs_scale=x_scale[:, c0 : c0 + n],
+                start=True,
+                stop=True,
+            )
+            nc.scalar.activation(th[:, t, c0 : c0 + n], u[:, 0:n], ACT.Tanh, bias=zero_bias[:], scale=0.5)
+
+        def maps(t):
+            if t == 0:
+                first_product(0, 0, HALF, "bank0")
+                first_product(0, HALF, HALF, "bank1")
+            else:
+                first_product(t, 0, S, f"bank{t + 1}")
+            nc.scalar.activation(sq[:, t, :], th[:, t, :], ACT.Square)
+            nc.vector.tensor_scalar(window[t][:], sq[:, t, :], -1.0, gain[:, 0, t : t + 1], ADD, MULT)
+            nc.scalar.activation(
+                base[:, t, :], sq[:, t, :], ACT.Identity, bias=gain[:, 2, t : t + 1], scale=gain[:, 1, t : t + 1]
+            )
+
+        def gather_first(t, i, pool, tag):
+            c0, n = PIECES[i]
+            part = pool.tile([P, n], F32, name="part", tag=tag, align_bytes=64)
+            nc.vector.tensor_tensor(
+                part[:], window[t][:].indirect(n1_t[:, c0 // 16 : (c0 + n) // 16]), base[:, t, c0 : c0 + n], ADD
+            )
+            return part
+
+        def gather_second(t, i, part):
+            c0, n = PIECES[i]
+            nc.vector.tensor_tensor(
+                sums[i][:, t, :], window[t][:].indirect(n2_t[:, c0 // 16 : (c0 + n) // 16]), part[:], ADD
+            )
+
+        for t in range(PACK):
+            maps(t)
+            parts = [gather_first(t, i, ring, "part") for i in range(2)]
+            for i in range(2):
+                gather_second(t, i, parts[i])
+
+        nc.scalar.copy(*w2_views(1))
+        w2_codes = keep.tile([P, N], U32, name="w2_codes", align_bytes=64)
+        w2_scale = keep.tile([P, N], U8, name="w2_scale", align_bytes=64)
+        nc.vector.quantize_mx(w2_codes[:].bitcast(FP8X4), w2_scale[:], w2_bf[:].rearrange("p n t -> p (n t)"))
+
+        z_codes = keep.tile([P, S], U32, name="z_codes", align_bytes=64)
+        z_scale = keep.tile([P, S], U8, name="z_scale", align_bytes=64)
+        out_rows = out.rearrange("(a p) c -> p a c", p=P)
+
+        def quantise_z(i, copy):
+            c0, n = PIECES[i]
+            z_bf = keep.tile([P, n, PACK], BF16, name="z_bf", tag=f"z_bf{i}", align_bytes=64)
+            copy(
+                z_bf[:].rearrange("p (c i) t -> p c t i", i=4),
+                sums[i][:].rearrange("p t (c i) -> p c t i", i=4),
+            )
+            nc.vector.quantize_mx(
+                z_codes[:, c0 : c0 + n].bitcast(FP8X4), z_scale[:, c0 : c0 + n], z_bf[:].rearrange("p n t -> p (n t)")
+            )
+
+        def second_product(i, banks, copies):
+            c0, n = PIECES[i]
+            res = keep.tile([P, PACK, n], F32, name=f"res{i}", align_bytes=64)
+            per_bank = PACK // len(banks)
+            for b, bank in enumerate(banks):
+                acc = psum.tile([P, S], F32, name="acc", tag=bank)
+                for k in range(per_bank):
+                    a = b * per_bank + k
+                    nc.tensor.matmul_mx(
+                        acc[:, k * n : (k + 1) * n],
+                        lhsT=w2_codes[:, a * P : (a + 1) * P].bitcast(FP8X4),
+                        lhsT_scale=w2_scale[:, a * P : (a + 1) * P],
+                        rhs=z_codes[:, c0 : c0 + n].bitcast(FP8X4),
+                        rhs_scale=z_scale[:, c0 : c0 + n],
+                        start=True,
+                        stop=True,
+                    )
+                copies[b](
+                    res[:, b * per_bank : (b + 1) * per_bank, :].rearrange("p a c -> p (a c)"),
+                    acc[:, 0 : per_bank * n],
+                )
+            nc.sync.dma_start(out_rows[:, :, c0 : c0 + n], res[:])
+
+        quantise_z(0, nc.scalar.copy)
+        second_product(0, ("bank5", "bank6"), (nc.scalar.copy, nc.scalar.copy))
+        parts = [gather_first(0, 2, keep, "z_bf0"), gather_first(1, 2, ring, "part")]
+        gather_second(0, 2, parts[0])
+        gather_second(1, 2, parts[1])
+        quantise_z(1, nc.scalar.copy)
+        second_product(1, ("bank7",), (nc.scalar.copy,))
+        parts = [gather_first(2, 2, keep, "z_bf1"), gather_first(3, 2, ring, "part")]
+        gather_second(2, 2, parts[0])
+        gather_second(3, 2, parts[1])
+        quantise_z(2, nc.vector.tensor_copy)
+        second_product(2, ("bank0", "bank1"), (nc.scalar.copy, nc.vector.tensor_copy))

@@ -19,137 +19,156 @@ MULT = mybir.AluOpType.mult
 P = 128
 PACK = 4
 HALF = 256
-PIECES = ((0, 256), (256, 128), (384, 128))
+QUARTER = 128
+LEFT = slice(0, HALF)
+RIGHT = slice(HALF, S)
+THIRD = slice(HALF, HALF + QUARTER)
+FOURTH = slice(HALF + QUARTER, S)
 
 
 def tile_picked_cmlmap_none_p_kernel(tc, x_words, x_scales, w1, gn, w2, offs, n1, n2, out):
     nc = tc.nc
     with ExitStack() as ctx:
         keep = ctx.enter_context(tc.tile_pool(name="keep", bufs=1))
-        ring = ctx.enter_context(tc.tile_pool(name="ring", bufs=2))
         psum = ctx.enter_context(tc.psum_pool(name="psum", bufs=1))
+
+        def entries(lists, c0, n):
+            return lists[:, c0 // 16 : (c0 + n) // 16]
 
         offs_t = keep.tile([P, S // 16], U16, name="offs_t")
         n1_t = keep.tile([P, S // 16], U16, name="n1_t")
         n2_t = keep.tile([P, S // 16], U16, name="n2_t")
         gn_t = keep.tile([P, PACK], F32, name="gn_t")
-        words_all = keep.tile([P, T], U32, name="words_all", align_bytes=64)
+        words_all = keep.tile([P, T], U32, name="words_all", tag="words_all", align_bytes=64)
         scales_all = keep.tile([P, T], U8, name="scales_all", align_bytes=64)
-        w1_raw = [keep.tile([P, PACK, HALF], F32, name="w1_raw", tag=f"raw{h}", align_bytes=64) for h in range(2)]
-        w1_rows = w1.rearrange("(p j) c -> p j c", j=PACK)
-        w2_rows = w2.rearrange("(p j) c -> p j c", j=PACK)
-
-        zero = keep.tile([P, 1], F32, name="zero")
+        w1_raw = keep.tile([P, PACK, H], F32, name="w1_raw", align_bytes=64)
+        zero = keep.tile([P, 1], F32, name="zero", tag="w2_raw", align_bytes=64)
         zero_bias = keep.tile([P, 1], F32, name="zero_bias")
+
         nc.vector.memset(scales_all[:].bitcast(I32), 0)
         nc.vector.memset(zero[:], 0.0)
+        nc.sync.dma_start(offs_t[:], offs)
+        nc.scalar.dma_start(gn_t[:], gn.rearrange("(p t) o -> p (t o)", t=PACK))
+        nc.sync.dma_start(w1_raw[:], w1.rearrange("(p j) c -> p j c", j=PACK))
+        nc.sync.dma_start(n1_t[:], n1)
+        nc.sync.dma_start(words_all[:].bitcast(I32), x_words[0].rearrange("p n r -> p (n r)").bitcast(I32))
         for q in range(4):
             nc.scalar.dma_start(
                 scales_all[32 * q : 32 * q + 4, :].bitcast(I32),
                 x_scales[0, 4 * q : 4 * q + 4, :].bitcast(I32),
             )
-        nc.scalar.activation(zero_bias[:], zero[:], ACT.Tanh)
-
-        nc.sync.dma_start(w1_raw[0][:], w1_rows[:, :, 0:HALF])
-        nc.sync.dma_start(offs_t[:], offs)
-        nc.sync.dma_start(n1_t[:], n1)
         nc.sync.dma_start(n2_t[:], n2)
-        nc.sync.dma_start(w1_raw[1][:], w1_rows[:, :, HALF:H])
-        nc.sync.dma_start(words_all[:].bitcast(I32), x_words[0].rearrange("p n r -> p (n r)").bitcast(I32))
-        nc.sync.dma_start(gn_t[:], gn.rearrange("(p t) o -> p (t o)", t=PACK))
-
-        w1_bf = keep.tile([P, PACK, P, PACK], BF16, name="w1_bf", align_bytes=64)
-        m_half = HALF // PACK
-        nc.scalar.copy(
-            w1_bf[:, :, 0:m_half, :].rearrange("p t m j -> p m j t"),
-            w1_raw[0][:].rearrange("p j (m t) -> p m j t", t=PACK),
-        )
-        x_scale = keep.tile([P, S], U8, name="x_scale", align_bytes=64)
-        nc.vector.tensor_copy(x_scale[:], scales_all[:].indirect(offs_t[:]))
-        nc.vector.tensor_copy(
-            w1_bf[:, :, m_half:P, :].rearrange("p t m j -> p m j t"),
-            w1_raw[1][:].rearrange("p j (m t) -> p m j t", t=PACK),
-        )
-        w2_raw = [keep.tile([P, PACK, HALF], F32, name="w2_raw", tag=f"raw{h}", align_bytes=64) for h in range(2)]
-        for h in range(2):
-            nc.sync.dma_start(w2_raw[h][:], w2_rows[:, :, h * HALF : (h + 1) * HALF])
-        w1_codes = keep.tile([P, H], U32, name="w1_codes", align_bytes=64)
-        w1_scale = keep.tile([P, H], U8, name="w1_scale", align_bytes=64)
-        nc.vector.quantize_mx(w1_codes[:].bitcast(FP8X4), w1_scale[:], w1_bf[:].rearrange("p t m j -> p (t m j)"))
+        nc.scalar.activation(zero_bias[:], zero[:], ACT.Tanh)
+        w2_raw = keep.tile([P, PACK, N], F32, name="w2_raw", tag="w2_raw", align_bytes=64)
+        nc.sync.dma_start(w2_raw[:], w2.rearrange("(p j) c -> p j c", j=PACK))
 
         gain = keep.tile([P, 3, PACK], F32, name="gain")
-        nc.vector.tensor_scalar(gain[:, 0, :], gn_t[:], 0.35, None, MULT)
-        nc.vector.tensor_scalar(gain[:, 1, :], gn_t[:], -0.525, None, MULT)
-        nc.vector.tensor_scalar(gain[:, 2, :], gn_t[:], 0.525, None, MULT)
+        for k, factor in enumerate((0.35, -0.525, -0.175)):
+            nc.vector.tensor_scalar(gain[:, k, :], gn_t[:], factor, None, MULT)
+        x_scale = keep.tile([P, S], U8, name="x_scale", align_bytes=64)
+        nc.vector.tensor_copy(x_scale[:], scales_all[:].indirect(offs_t[:]))
 
+        w1_view = w1_raw[:].rearrange("p j (m t) -> p m j t", t=PACK)
+        w1_bf = [keep.tile([P, 2, P, PACK], BF16, name=f"w1_bf{u}", align_bytes=64) for u in range(2)]
+        for u in range(2):
+            nc.scalar.copy(w1_bf[u][:].rearrange("p t m j -> p m j t"), w1_view[:, :, :, 2 * u : 2 * u + 2])
+        w1_scale = keep.tile([P, H], U8, name="w1_scale", align_bytes=64)
+
+        def quantise_w1(u, tag):
+            codes = keep.tile([P, HALF], U32, name="w1_codes", tag=tag, align_bytes=64)
+            nc.vector.quantize_mx(
+                codes[:].bitcast(FP8X4),
+                w1_scale[:, u * HALF : (u + 1) * HALF],
+                w1_bf[u][:].rearrange("p t m j -> p (t m j)"),
+            )
+            return codes
+
+        w1_codes = [quantise_w1(0, "w1_codes")]
         x_codes = keep.tile([P, S], U32, name="x_codes", align_bytes=64)
         for h in range(2):
             nc.vector.tensor_copy(
-                x_codes[:, h * HALF : (h + 1) * HALF],
-                words_all[:].indirect(offs_t[:, h * HALF // 16 : (h + 1) * HALF // 16]),
+                x_codes[:, h * HALF : (h + 1) * HALF], words_all[:].indirect(entries(offs_t, h * HALF, HALF))
             )
+        w1_codes.append(quantise_w1(1, "words_all"))
 
-        w2_bf = keep.tile([P, N, PACK], BF16, name="w2_bf", align_bytes=64)
-
-        def w2_views(h):
-            dst = w2_bf[:, h * HALF : (h + 1) * HALF, :].rearrange("p (c i) t -> p c t i", i=4)
-            src = w2_raw[h][:].rearrange("p t (c i) -> p c t i", i=4)
-            return dst, src
-
-        nc.vector.tensor_copy(*w2_views(0))
-
-        th = keep.tile([P, PACK, S], F32, name="th")
-        sq = keep.tile([P, PACK, S], F32, name="sq")
-        base = keep.tile([P, PACK, S], F32, name="base")
-        window = [keep.tile([P, S], F32, name=f"window{t}", align_bytes=64) for t in range(PACK)]
-        sums = [keep.tile([P, PACK, n], F32, name=f"sums{i}", align_bytes=64) for i, (c, n) in enumerate(PIECES)]
-
-        def first_product(t, c0, n, bank):
-            u = psum.tile([P, S], F32, name="u", tag=bank)
+        def first_product(t, cols, bank):
+            u = psum.tile([P, cols.stop - cols.start], F32, name="u", tag=bank)
             nc.tensor.matmul_mx(
-                u[:, 0:n],
-                lhsT=w1_codes[:, t * P : (t + 1) * P].bitcast(FP8X4),
+                u[:],
+                lhsT=w1_codes[t // 2][:, t % 2 * P : (t % 2 + 1) * P].bitcast(FP8X4),
                 lhsT_scale=w1_scale[:, t * P : (t + 1) * P],
-                rhs=x_codes[:, c0 : c0 + n].bitcast(FP8X4),
-                rhs_scale=x_scale[:, c0 : c0 + n],
+                rhs=x_codes[:, cols].bitcast(FP8X4),
+                rhs_scale=x_scale[:, cols],
                 start=True,
                 stop=True,
             )
-            nc.scalar.activation(th[:, t, c0 : c0 + n], u[:, 0:n], ACT.Tanh, bias=zero_bias[:], scale=0.5)
+            return u
 
-        def maps(t):
-            if t == 0:
-                first_product(0, 0, HALF, "bank0")
-                first_product(0, HALF, HALF, "bank1")
+        window = [keep.tile([P, S], F32, name=f"window{t}", align_bytes=64) for t in range(PACK)]
+        base = [keep.tile([P, S], F32, name="base", tag=f"base{t}", align_bytes=64) for t in range(PACK)]
+        part_left = [keep.tile([P, HALF], F32, name=f"part_left{t}", align_bytes=64) for t in range(PACK)]
+        part_right = [keep.tile([P, HALF], F32, name=f"part_right{t}", align_bytes=64) for t in range(PACK)]
+        sums_a = keep.tile([P, PACK, HALF], F32, name="sums_a", tag="sums_a", align_bytes=64)
+
+        def add_first(t, cols, part):
+            nc.vector.tensor_tensor(
+                part[t][:], window[t][:].indirect(entries(n1_t, cols.start, HALF)), base[t][:, cols], ADD
+            )
+
+        def add_second(t, c0, n, part, sums):
+            nc.vector.tensor_tensor(sums, window[t][:].indirect(entries(n2_t, c0, n)), part, ADD)
+
+        def base_from_window(cols):
+            nc.vector.tensor_scalar(base[0][:, cols], window[0][:, cols], -1.5, gain[:, 2, 0:1], MULT, ADD)
+
+        th0 = keep.tile([P, S], F32, name="th0", align_bytes=64)
+        nc.scalar.activation(th0[:, LEFT], first_product(0, LEFT, "bank0")[:], ACT.Tanh, bias=zero_bias[:], scale=0.5)
+        for cols, bank in ((THIRD, "bank1"), (FOURTH, "bank5")):
+            nc.scalar.activation(th0[:, cols], first_product(0, cols, bank)[:], ACT.Tanh, scale=0.5)
+        for cols in (LEFT, THIRD, FOURTH):
+            nc.vector.scalar_tensor_tensor(
+                window[0][:, cols], th0[:, cols], gain[:, 0, 0:1], th0[:, cols], MULT, MULT
+            )
+            if cols is LEFT:
+                base_from_window(LEFT)
+        add_first(0, LEFT, part_left)
+        base_from_window(RIGHT)
+        add_first(0, RIGHT, part_right)
+        add_second(0, 0, HALF, part_left[0][:], sums_a[:, 0, :])
+
+        for t in range(1, PACK):
+            u = first_product(t, slice(0, S), f"bank{t + 1}")
+            th = keep.tile([P, S], F32, name="th", tag="th", align_bytes=64)
+            sq = keep.tile([P, S], F32, name="sq", tag=f"sq{t}", align_bytes=64)
+            for cols in (LEFT, RIGHT):
+                nc.scalar.activation(th[:, cols], u[:, cols], ACT.Tanh, scale=0.5)
+            for cols in (LEFT, RIGHT):
+                nc.scalar.activation(sq[:, cols], th[:, cols], ACT.Square)
+
+            def base_from_square(cols):
+                nc.scalar.activation(
+                    base[t][:, cols], sq[:, cols], ACT.Identity, bias=gain[:, 2, t : t + 1], scale=gain[:, 1, t : t + 1]
+                )
+
+            base_from_square(LEFT)
+            if t == 1:
+                nc.vector.tensor_scalar(window[t][:], sq[:], gain[:, 0, t : t + 1], None, MULT)
             else:
-                first_product(t, 0, S, f"bank{t + 1}")
-            nc.scalar.activation(sq[:, t, :], th[:, t, :], ACT.Square)
-            nc.vector.tensor_scalar(window[t][:], sq[:, t, :], -1.0, gain[:, 0, t : t + 1], ADD, MULT)
-            nc.scalar.activation(
-                base[:, t, :], sq[:, t, :], ACT.Identity, bias=gain[:, 2, t : t + 1], scale=gain[:, 1, t : t + 1]
-            )
+                nc.scalar.activation(window[t][:], sq[:], ACT.Copy, scale=gain[:, 0, t : t + 1])
+            base_from_square(RIGHT)
+            add_first(t, LEFT, part_left)
+            add_first(t, RIGHT, part_right)
+            add_second(t, 0, HALF, part_left[t][:], sums_a[:, t, :])
 
-        def gather_first(t, i, pool, tag):
-            c0, n = PIECES[i]
-            part = pool.tile([P, n], F32, name="part", tag=tag, align_bytes=64)
-            nc.vector.tensor_tensor(
-                part[:], window[t][:].indirect(n1_t[:, c0 // 16 : (c0 + n) // 16]), base[:, t, c0 : c0 + n], ADD
-            )
-            return part
-
-        def gather_second(t, i, part):
-            c0, n = PIECES[i]
-            nc.vector.tensor_tensor(
-                sums[i][:, t, :], window[t][:].indirect(n2_t[:, c0 // 16 : (c0 + n) // 16]), part[:], ADD
-            )
-
+        sums_b = keep.tile([P, PACK, QUARTER], F32, name="sums_b", tag="base3", align_bytes=64)
         for t in range(PACK):
-            maps(t)
-            parts = [gather_first(t, i, ring, "part") for i in range(2)]
-            for i in range(2):
-                gather_second(t, i, parts[i])
+            add_second(t, HALF, QUARTER, part_right[t][:, 0:QUARTER], sums_b[:, t, :])
 
-        nc.scalar.copy(*w2_views(1))
+        def interleave(copy, dst, src):
+            copy(dst.rearrange("p (c i) t -> p c t i", i=4), src.rearrange("p t (c i) -> p c t i", i=4))
+
+        w2_bf = keep.tile([P, N, PACK], BF16, name="w2_bf", tag="sq3", align_bytes=64)
+        interleave(nc.scalar.copy, w2_bf[:], w2_raw[:])
         w2_codes = keep.tile([P, N], U32, name="w2_codes", align_bytes=64)
         w2_scale = keep.tile([P, N], U8, name="w2_scale", align_bytes=64)
         nc.vector.quantize_mx(w2_codes[:].bitcast(FP8X4), w2_scale[:], w2_bf[:].rearrange("p n t -> p (n t)"))
@@ -158,23 +177,16 @@ def tile_picked_cmlmap_none_p_kernel(tc, x_words, x_scales, w1, gn, w2, offs, n1
         z_scale = keep.tile([P, S], U8, name="z_scale", align_bytes=64)
         out_rows = out.rearrange("(a p) c -> p a c", p=P)
 
-        def quantise_z(i, copy):
-            c0, n = PIECES[i]
-            z_bf = keep.tile([P, n, PACK], BF16, name="z_bf", tag=f"z_bf{i}", align_bytes=64)
-            copy(
-                z_bf[:].rearrange("p (c i) t -> p c t i", i=4),
-                sums[i][:].rearrange("p t (c i) -> p c t i", i=4),
-            )
+        def quantise_z(c0, n, z_bf):
             nc.vector.quantize_mx(
                 z_codes[:, c0 : c0 + n].bitcast(FP8X4), z_scale[:, c0 : c0 + n], z_bf[:].rearrange("p n t -> p (n t)")
             )
 
-        def second_product(i, banks, copies):
-            c0, n = PIECES[i]
-            res = keep.tile([P, PACK, n], F32, name=f"res{i}", align_bytes=64)
-            per_bank = PACK // len(banks)
-            for b, bank in enumerate(banks):
-                acc = psum.tile([P, S], F32, name="acc", tag=bank)
+        def second_product(c0, n, ways):
+            per_bank = PACK // len(ways)
+            for b, (bank, copy, queue) in enumerate(ways):
+                acc = psum.tile([P, per_bank * n], F32, name="acc", tag=bank)
+                res = keep.tile([P, per_bank, n], F32, name=f"res{c0}_{b}", align_bytes=64)
                 for k in range(per_bank):
                     a = b * per_bank + k
                     nc.tensor.matmul_mx(
@@ -186,21 +198,26 @@ def tile_picked_cmlmap_none_p_kernel(tc, x_words, x_scales, w1, gn, w2, offs, n1
                         start=True,
                         stop=True,
                     )
-                copies[b](
-                    res[:, b * per_bank : (b + 1) * per_bank, :].rearrange("p a c -> p (a c)"),
-                    acc[:, 0 : per_bank * n],
-                )
-            nc.sync.dma_start(out_rows[:, :, c0 : c0 + n], res[:])
+                copy(res[:].rearrange("p a c -> p (a c)"), acc[:])
+                queue.dma_start(out_rows[:, b * per_bank : (b + 1) * per_bank, c0 : c0 + n], res[:])
 
-        quantise_z(0, nc.scalar.copy)
-        second_product(0, ("bank5", "bank6"), (nc.scalar.copy, nc.scalar.copy))
-        parts = [gather_first(0, 2, keep, "z_bf0"), gather_first(1, 2, ring, "part")]
-        gather_second(0, 2, parts[0])
-        gather_second(1, 2, parts[1])
-        quantise_z(1, nc.scalar.copy)
-        second_product(1, ("bank7",), (nc.scalar.copy,))
-        parts = [gather_first(2, 2, keep, "z_bf1"), gather_first(3, 2, ring, "part")]
-        gather_second(2, 2, parts[0])
-        gather_second(3, 2, parts[1])
-        quantise_z(2, nc.vector.tensor_copy)
-        second_product(2, ("bank0", "bank1"), (nc.scalar.copy, nc.vector.tensor_copy))
+        z_a = keep.tile([P, HALF, PACK], BF16, name="z_a", align_bytes=64)
+        interleave(nc.scalar.copy, z_a[:], sums_a[:])
+        quantise_z(0, HALF, z_a)
+        second_product(0, HALF, (("bank5", nc.scalar.copy, nc.sync), ("bank6", nc.scalar.copy, nc.sync)))
+
+        z_b = keep.tile([P, QUARTER, PACK], BF16, name="z_b", align_bytes=64)
+        interleave(nc.scalar.copy, z_b[:], sums_b[:])
+        quantise_z(HALF, QUARTER, z_b)
+        second_product(HALF, QUARTER, (("bank7", nc.scalar.copy, nc.sync),))
+
+        last = HALF + QUARTER
+        z_c = keep.tile([P, QUARTER, PACK], BF16, name="z_c", align_bytes=64)
+        for u, (tag, copy) in enumerate((("w2_raw", nc.scalar.copy), ("sums_a", nc.vector.tensor_copy))):
+            sums_c = keep.tile([P, 2, QUARTER], F32, name="sums_c", tag=tag, align_bytes=64)
+            for k in range(2):
+                t = 2 * u + k
+                add_second(t, last, QUARTER, part_right[t][:, QUARTER:HALF], sums_c[:, k, :])
+            interleave(copy, z_c[:, :, 2 * u : 2 * u + 2], sums_c[:])
+        quantise_z(last, QUARTER, z_c)
+        second_product(last, QUARTER, (("bank0", nc.scalar.copy, nc.scalar), ("bank1", nc.vector.tensor_copy, nc.sync)))

@@ -137,11 +137,15 @@ def tile_picked_cmlmap_none_p_kernel(tc, x_words, x_scales, w1, gn, w2, offs, n1
         add_second(0, 0, HALF, part_left[0][:], sums_a[:, 0, :])
 
         for t in range(1, PACK):
-            u = first_product(t, slice(0, S), f"bank{t + 1}")
+            if t == 1:
+                halves = [first_product(t, LEFT, "bank2")[:], first_product(t, RIGHT, "bank6")[:]]
+            else:
+                u = first_product(t, slice(0, S), f"bank{t + 1}")
+                halves = [u[:, LEFT], u[:, RIGHT]]
             th = keep.tile([P, S], F32, name="th", tag="th", align_bytes=64)
             sq = keep.tile([P, S], F32, name="sq", tag=f"sq{t}", align_bytes=64)
-            for cols in (LEFT, RIGHT):
-                nc.scalar.activation(th[:, cols], u[:, cols], ACT.Tanh, scale=0.5)
+            for cols, half in zip((LEFT, RIGHT), halves):
+                nc.scalar.activation(th[:, cols], half, ACT.Tanh, scale=0.5)
             for cols in (LEFT, RIGHT):
                 nc.scalar.activation(sq[:, cols], th[:, cols], ACT.Square)
 
@@ -182,34 +186,36 @@ def tile_picked_cmlmap_none_p_kernel(tc, x_words, x_scales, w1, gn, w2, offs, n1
                 z_codes[:, c0 : c0 + n].bitcast(FP8X4), z_scale[:, c0 : c0 + n], z_bf[:].rearrange("p n t -> p (n t)")
             )
 
-        def second_product(c0, n, ways):
-            per_bank = PACK // len(ways)
-            for b, (bank, copy, queue) in enumerate(ways):
+        def output_block(a, c0, n, acc):
+            nc.tensor.matmul_mx(
+                acc,
+                lhsT=w2_codes[:, a * P : (a + 1) * P].bitcast(FP8X4),
+                lhsT_scale=w2_scale[:, a * P : (a + 1) * P],
+                rhs=z_codes[:, c0 : c0 + n].bitcast(FP8X4),
+                rhs_scale=z_scale[:, c0 : c0 + n],
+                start=True,
+                stop=True,
+            )
+
+        def second_product(c0, n, banks):
+            per_bank = PACK // len(banks)
+            for b, bank in enumerate(banks):
                 acc = psum.tile([P, per_bank * n], F32, name="acc", tag=bank)
                 res = keep.tile([P, per_bank, n], F32, name=f"res{c0}_{b}", align_bytes=64)
                 for k in range(per_bank):
-                    a = b * per_bank + k
-                    nc.tensor.matmul_mx(
-                        acc[:, k * n : (k + 1) * n],
-                        lhsT=w2_codes[:, a * P : (a + 1) * P].bitcast(FP8X4),
-                        lhsT_scale=w2_scale[:, a * P : (a + 1) * P],
-                        rhs=z_codes[:, c0 : c0 + n].bitcast(FP8X4),
-                        rhs_scale=z_scale[:, c0 : c0 + n],
-                        start=True,
-                        stop=True,
-                    )
-                copy(res[:].rearrange("p a c -> p (a c)"), acc[:])
-                queue.dma_start(out_rows[:, b * per_bank : (b + 1) * per_bank, c0 : c0 + n], res[:])
+                    output_block(b * per_bank + k, c0, n, acc[:, k * n : (k + 1) * n])
+                nc.scalar.copy(res[:].rearrange("p a c -> p (a c)"), acc[:])
+                nc.sync.dma_start(out_rows[:, b * per_bank : (b + 1) * per_bank, c0 : c0 + n], res[:])
 
         z_a = keep.tile([P, HALF, PACK], BF16, name="z_a", align_bytes=64)
         interleave(nc.scalar.copy, z_a[:], sums_a[:])
         quantise_z(0, HALF, z_a)
-        second_product(0, HALF, (("bank5", nc.scalar.copy, nc.sync), ("bank6", nc.scalar.copy, nc.sync)))
+        second_product(0, HALF, ("bank5", "bank6"))
 
         z_b = keep.tile([P, QUARTER, PACK], BF16, name="z_b", align_bytes=64)
         interleave(nc.scalar.copy, z_b[:], sums_b[:])
         quantise_z(HALF, QUARTER, z_b)
-        second_product(HALF, QUARTER, (("bank7", nc.scalar.copy, nc.sync),))
+        second_product(HALF, QUARTER, ("bank7",))
 
         last = HALF + QUARTER
         z_c = keep.tile([P, QUARTER, PACK], BF16, name="z_c", align_bytes=64)
@@ -220,4 +226,11 @@ def tile_picked_cmlmap_none_p_kernel(tc, x_words, x_scales, w1, gn, w2, offs, n1
                 add_second(t, last, QUARTER, part_right[t][:, QUARTER:HALF], sums_c[:, k, :])
             interleave(copy, z_c[:, :, 2 * u : 2 * u + 2], sums_c[:])
         quantise_z(last, QUARTER, z_c)
-        second_product(last, QUARTER, (("bank0", nc.scalar.copy, nc.scalar), ("bank1", nc.vector.tensor_copy, nc.sync)))
+        res_c = [keep.tile([P, 2, QUARTER], F32, name=f"res_c{e}", align_bytes=64) for e in range(2)]
+        for a in range(PACK):
+            acc = psum.tile([P, QUARTER], F32, name="acc", tag=f"bank{a}")
+            output_block(a, last, QUARTER, acc[:])
+            (nc.vector.tensor_copy, nc.scalar.copy)[a % 2](res_c[a % 2][:, a // 2, :], acc[:])
+        pairs = out.rearrange("(h e p) c -> e p h c", e=2, p=P)
+        nc.sync.dma_start(pairs[0][:, :, last:S], res_c[0][:])
+        nc.scalar.dma_start(pairs[1][:, :, last:S], res_c[1][:])

@@ -186,51 +186,44 @@ def tile_picked_cmlmap_none_p_kernel(tc, x_words, x_scales, w1, gn, w2, offs, n1
                 z_codes[:, c0 : c0 + n].bitcast(FP8X4), z_scale[:, c0 : c0 + n], z_bf[:].rearrange("p n t -> p (n t)")
             )
 
-        def output_block(a, c0, n, acc):
-            nc.tensor.matmul_mx(
-                acc,
-                lhsT=w2_codes[:, a * P : (a + 1) * P].bitcast(FP8X4),
-                lhsT_scale=w2_scale[:, a * P : (a + 1) * P],
-                rhs=z_codes[:, c0 : c0 + n].bitcast(FP8X4),
-                rhs_scale=z_scale[:, c0 : c0 + n],
-                start=True,
-                stop=True,
-            )
-
-        def second_product(c0, n, banks):
-            per_bank = PACK // len(banks)
-            for b, bank in enumerate(banks):
+        def second_product(c0, n, ways):
+            per_bank = PACK // len(ways)
+            for b, (bank, copy, queue) in enumerate(ways):
                 acc = psum.tile([P, per_bank * n], F32, name="acc", tag=bank)
                 res = keep.tile([P, per_bank, n], F32, name=f"res{c0}_{b}", align_bytes=64)
                 for k in range(per_bank):
-                    output_block(b * per_bank + k, c0, n, acc[:, k * n : (k + 1) * n])
-                nc.scalar.copy(res[:].rearrange("p a c -> p (a c)"), acc[:])
-                nc.sync.dma_start(out_rows[:, b * per_bank : (b + 1) * per_bank, c0 : c0 + n], res[:])
-
-        z_a = keep.tile([P, HALF, PACK], BF16, name="z_a", align_bytes=64)
-        interleave(nc.scalar.copy, z_a[:], sums_a[:])
-        quantise_z(0, HALF, z_a)
-        second_product(0, HALF, ("bank5", "bank6"))
-
-        z_b = keep.tile([P, QUARTER, PACK], BF16, name="z_b", align_bytes=64)
-        interleave(nc.scalar.copy, z_b[:], sums_b[:])
-        quantise_z(HALF, QUARTER, z_b)
-        second_product(HALF, QUARTER, ("bank7",))
+                    a = b * per_bank + k
+                    nc.tensor.matmul_mx(
+                        acc[:, k * n : (k + 1) * n],
+                        lhsT=w2_codes[:, a * P : (a + 1) * P].bitcast(FP8X4),
+                        lhsT_scale=w2_scale[:, a * P : (a + 1) * P],
+                        rhs=z_codes[:, c0 : c0 + n].bitcast(FP8X4),
+                        rhs_scale=z_scale[:, c0 : c0 + n],
+                        start=True,
+                        stop=True,
+                    )
+                copy(res[:].rearrange("p a c -> p (a c)"), acc[:])
+                queue.dma_start(out_rows[:, b * per_bank : (b + 1) * per_bank, c0 : c0 + n], res[:])
 
         last = HALF + QUARTER
+        z_a = keep.tile([P, HALF, PACK], BF16, name="z_a", align_bytes=64)
+        z_b = keep.tile([P, QUARTER, PACK], BF16, name="z_b", align_bytes=64)
         z_c = keep.tile([P, QUARTER, PACK], BF16, name="z_c", align_bytes=64)
-        for u, (tag, copy) in enumerate((("w2_raw", nc.scalar.copy), ("sums_a", nc.vector.tensor_copy))):
+
+        def last_pair(u, tag, copy):
             sums_c = keep.tile([P, 2, QUARTER], F32, name="sums_c", tag=tag, align_bytes=64)
             for k in range(2):
                 t = 2 * u + k
                 add_second(t, last, QUARTER, part_right[t][:, QUARTER:HALF], sums_c[:, k, :])
             interleave(copy, z_c[:, :, 2 * u : 2 * u + 2], sums_c[:])
+
+        interleave(nc.scalar.copy, z_a[:], sums_a[:])
+        quantise_z(0, HALF, z_a)
+        interleave(nc.scalar.copy, z_b[:], sums_b[:])
+        quantise_z(HALF, QUARTER, z_b)
+        last_pair(0, "w2_raw", nc.scalar.copy)
+        second_product(0, HALF, (("bank5", nc.scalar.copy, nc.sync), ("bank6", nc.scalar.copy, nc.sync)))
+        second_product(HALF, QUARTER, (("bank7", nc.scalar.copy, nc.sync),))
+        last_pair(1, "sums_a", nc.vector.tensor_copy)
         quantise_z(last, QUARTER, z_c)
-        res_c = [keep.tile([P, 2, QUARTER], F32, name=f"res_c{e}", align_bytes=64) for e in range(2)]
-        for a in range(PACK):
-            acc = psum.tile([P, QUARTER], F32, name="acc", tag=f"bank{a}")
-            output_block(a, last, QUARTER, acc[:])
-            (nc.vector.tensor_copy, nc.scalar.copy)[a % 2](res_c[a % 2][:, a // 2, :], acc[:])
-        pairs = out.rearrange("(h e p) c -> e p h c", e=2, p=P)
-        nc.sync.dma_start(pairs[0][:, :, last:S], res_c[0][:])
-        nc.scalar.dma_start(pairs[1][:, :, last:S], res_c[1][:])
+        second_product(last, QUARTER, (("bank0", nc.vector.tensor_copy, nc.sync), ("bank1", nc.scalar.copy, nc.scalar)))

@@ -221,9 +221,9 @@ def tile_picked_cmlmap_none_p_kernel(tc, x_words, x_scales, w1, gn, w2, offs, n1
         quantise_z(0, HALF, z_a)
         interleave(nc.scalar.copy, z_b[:], sums_b[:])
         quantise_z(HALF, QUARTER, z_b)
-        last_pair(0, "w2_raw", nc.scalar.copy)
+        last_pair(0, "sums_a", nc.scalar.copy)
         second_product(0, HALF, (("bank5", nc.scalar.copy, nc.sync), ("bank6", nc.scalar.copy, nc.sync)))
         second_product(HALF, QUARTER, (("bank7", nc.scalar.copy, nc.sync),))
-        last_pair(1, "sums_a", nc.vector.tensor_copy)
+        last_pair(1, "base3", nc.vector.tensor_copy)
         quantise_z(last, QUARTER, z_c)
         second_product(last, QUARTER, (("bank0", nc.vector.tensor_copy, nc.sync), ("bank1", nc.scalar.copy, nc.scalar)))

from contextlib import ExitStack

import concourse.mybir as mybir

K, T, S, H, N = 512, 2048, 512, 512, 512
FLOPS = 2 * K * H * S + 2 * H * N * S

F32 = mybir.dt.float32
BF16 = mybir.dt.bfloat16
I32 = mybir.dt.int32
U32 = mybir.dt.uint32
U16 = mybir.dt.uint16
U8 = mybir.dt.uint8
FP8X4 = mybir.dt.float8_e4m3fn_x4
ACT = mybir.ActivationFunctionType
ADD = mybir.AluOpType.add
MULT = mybir.AluOpType.mult

P = 128
PACK = 4
HALF = 256
QUARTER = 128
LEFT = slice(0, HALF)
RIGHT = slice(HALF, S)
THIRD = slice(HALF, HALF + QUARTER)
FOURTH = slice(HALF + QUARTER, S)


def tile_picked_cmlmap_none_p_kernel(tc, x_words, x_scales, w1, gn, w2, offs, n1, n2, out):
    nc = tc.nc
    with ExitStack() as ctx:
        keep = ctx.enter_context(tc.tile_pool(name="keep", bufs=1))
        psum = ctx.enter_context(tc.psum_pool(name="psum", bufs=1))

        def entries(lists, c0, n):
            return lists[:, c0 // 16 : (c0 + n) // 16]

        offs_t = keep.tile([P, S // 16], U16, name="offs_t")
        n1_t = keep.tile([P, S // 16], U16, name="n1_t")
        n2_t = keep.tile([P, S // 16], U16, name="n2_t")
        gn_t = keep.tile([P, PACK], F32, name="gn_t")
        words_all = keep.tile([P, T], U32, name="words_all", tag="words_all", align_bytes=64)
        scales_all = keep.tile([P, T], U8, name="scales_all", align_bytes=64)
        w1_raw = keep.tile([P, PACK, H], F32, name="w1_raw", align_bytes=64)
        zero = keep.tile([P, 1], F32, name="zero", tag="w2_raw", align_bytes=64)
        zero_bias = keep.tile([P, 1], F32, name="zero_bias")

        nc.vector.memset(scales_all[:].bitcast(I32), 0)
        nc.vector.memset(zero[:], 0.0)
        nc.sync.dma_start(offs_t[:], offs)
        nc.scalar.dma_start(gn_t[:], gn.rearrange("(p t) o -> p (t o)", t=PACK))
        nc.sync.dma_start(w1_raw[:], w1.rearrange("(p j) c -> p j c", j=PACK))
        nc.sync.dma_start(n1_t[:], n1)
        nc.sync.dma_start(words_all[:].bitcast(I32), x_words[0].rearrange("p n r -> p (n r)").bitcast(I32))
        for q in range(4):
            nc.scalar.dma_start(
                scales_all[32 * q : 32 * q + 4, :].bitcast(I32),
                x_scales[0, 4 * q : 4 * q + 4, :].bitcast(I32),
            )
        nc.sync.dma_start(n2_t[:], n2)
        nc.scalar.activation(zero_bias[:], zero[:], ACT.Tanh)
        w2_raw = keep.tile([P, PACK, N], F32, name="w2_raw", tag="w2_raw", align_bytes=64)
        nc.sync.dma_start(w2_raw[:], w2.rearrange("(p j) c -> p j c", j=PACK))

        gain = keep.tile([P, 3, PACK], F32, name="gain")
        for k, factor in enumerate((0.35, -0.525, -0.175)):
            nc.vector.tensor_scalar(gain[:, k, :], gn_t[:], factor, None, MULT)
        x_scale = keep.tile([P, S], U8, name="x_scale", align_bytes=64)
        nc.vector.tensor_copy(x_scale[:], scales_all[:].indirect(offs_t[:]))

        w1_view = w1_raw[:].rearrange("p j (m t) -> p m j t", t=PACK)
        w1_bf = [keep.tile([P, 2, P, PACK], BF16, name=f"w1_bf{u}", align_bytes=64) for u in range(2)]
        for u in range(2):
            nc.scalar.copy(w1_bf[u][:].rearrange("p t m j -> p m j t"), w1_view[:, :, :, 2 * u : 2 * u + 2])
        w1_scale = keep.tile([P, H], U8, name="w1_scale", align_bytes=64)

        def quantise_w1(u, tag):
            codes = keep.tile([P, HALF], U32, name="w1_codes", tag=tag, align_bytes=64)
            nc.vector.quantize_mx(
                codes[:].bitcast(FP8X4),
                w1_scale[:, u * HALF : (u + 1) * HALF],
                w1_bf[u][:].rearrange("p t m j -> p (t m j)"),
            )
            return codes

        w1_codes = [quantise_w1(0, "w1_codes")]
        x_codes = keep.tile([P, S], U32, name="x_codes", align_bytes=64)
        for h in range(2):
            nc.vector.tensor_copy(
                x_codes[:, h * HALF : (h + 1) * HALF], words_all[:].indirect(entries(offs_t, h * HALF, HALF))
            )
        w1_codes.append(quantise_w1(1, "words_all"))

        def first_product(t, cols, bank):
            u = psum.tile([P, cols.stop - cols.start], F32, name="u", tag=bank)
            nc.tensor.matmul_mx(
                u[:],
                lhsT=w1_codes[t // 2][:, t % 2 * P : (t % 2 + 1) * P].bitcast(FP8X4),
                lhsT_scale=w1_scale[:, t * P : (t + 1) * P],
                rhs=x_codes[:, cols].bitcast(FP8X4),
                rhs_scale=x_scale[:, cols],
                start=True,
                stop=True,
            )
            return u

        window = [keep.tile([P, S], F32, name=f"window{t}", align_bytes=64) for t in range(PACK)]
        base = [keep.tile([P, S], F32, name="base", tag=f"base{t}", align_bytes=64) for t in range(PACK)]
        part_left = [keep.tile([P, HALF], F32, name=f"part_left{t}", align_bytes=64) for t in range(PACK)]
        part_right = [keep.tile([P, HALF], F32, name=f"part_right{t}", align_bytes=64) for t in range(PACK)]
        sums_a = keep.tile([P, PACK, HALF], F32, name="sums_a", tag="sums_a", align_bytes=64)

        def add_first(t, cols, part):
            nc.vector.tensor_tensor(
                part[t][:], window[t][:].indirect(entries(n1_t, cols.start, HALF)), base[t][:, cols], ADD
            )

        def add_second(t, c0, n, part, sums):
            nc.vector.tensor_tensor(sums, window[t][:].indirect(entries(n2_t, c0, n)), part, ADD)

        def base_from_window(cols):
            nc.vector.tensor_scalar(base[0][:, cols], window[0][:, cols], -1.5, gain[:, 2, 0:1], MULT, ADD)

        th0 = keep.tile([P, S], F32, name="th0", align_bytes=64)
        nc.scalar.activation(th0[:, LEFT], first_product(0, LEFT, "bank0")[:], ACT.Tanh, bias=zero_bias[:], scale=0.5)
        for cols, bank in ((THIRD, "bank1"), (FOURTH, "bank5")):
            nc.scalar.activation(th0[:, cols], first_product(0, cols, bank)[:], ACT.Tanh, scale=0.5)
        for cols in (LEFT, THIRD, FOURTH):
            nc.vector.scalar_tensor_tensor(
                window[0][:, cols], th0[:, cols], gain[:, 0, 0:1], th0[:, cols], MULT, MULT
            )
            if cols is LEFT:
                base_from_window(LEFT)
        add_first(0, LEFT, part_left)
        base_from_window(RIGHT)
        add_first(0, RIGHT, part_right)
        add_second(0, 0, HALF, part_left[0][:], sums_a[:, 0, :])

        for t in range(1, PACK):
            if t == 1:
                halves = [first_product(t, LEFT, "bank2")[:], first_product(t, RIGHT, "bank6")[:]]
            else:
                u = first_product(t, slice(0, S), f"bank{t + 1}")
                halves = [u[:, LEFT], u[:, RIGHT]]
            th = keep.tile([P, S], F32, name="th", tag="th", align_bytes=64)
            sq = keep.tile([P, S], F32, name="sq", tag=f"sq{t}", align_bytes=64)
            for cols, half in zip((LEFT, RIGHT), halves):
                nc.scalar.activation(th[:, cols], half, ACT.Tanh, scale=0.5)
            for cols in (LEFT, RIGHT):
                nc.scalar.activation(sq[:, cols], th[:, cols], ACT.Square)

            def base_from_square(cols):
                nc.scalar.activation(
                    base[t][:, cols], sq[:, cols], ACT.Identity, bias=gain[:, 2, t : t + 1], scale=gain[:, 1, t : t + 1]
                )

            base_from_square(LEFT)
            if t == 1:
                nc.vector.tensor_scalar(window[t][:], sq[:], gain[:, 0, t : t + 1], None, MULT)
            else:
                nc.scalar.activation(window[t][:], sq[:], ACT.Copy, scale=gain[:, 0, t : t + 1])
            base_from_square(RIGHT)
            add_first(t, LEFT, part_left)
            add_first(t, RIGHT, part_right)
            add_second(t, 0, HALF, part_left[t][:], sums_a[:, t, :])

        sums_b = keep.tile([P, PACK, QUARTER], F32, name="sums_b", tag="base3", align_bytes=64)
        for t in range(PACK):
            add_second(t, HALF, QUARTER, part_right[t][:, 0:QUARTER], sums_b[:, t, :])

        def interleave(copy, dst, src):
            copy(dst.rearrange("p (c i) t -> p c t i", i=4), src.rearrange("p t (c i) -> p c t i", i=4))

        w2_bf = keep.tile([P, N, PACK], BF16, name="w2_bf", tag="sq3", align_bytes=64)
        interleave(nc.scalar.copy, w2_bf[:], w2_raw[:])
        w2_codes = keep.tile([P, N], U32, name="w2_codes", align_bytes=64)
        w2_scale = keep.tile([P, N], U8, name="w2_scale", align_bytes=64)
        nc.vector.quantize_mx(w2_codes[:].bitcast(FP8X4), w2_scale[:], w2_bf[:].rearrange("p n t -> p (n t)"))

        z_codes = keep.tile([P, S], U32, name="z_codes", align_bytes=64)
        z_scale = keep.tile([P, S], U8, name="z_scale", align_bytes=64)
        out_rows = out.rearrange("(a p) c -> p a c", p=P)

        def quantise_z(c0, n, z_bf):
            nc.vector.quantize_mx(
                z_codes[:, c0 : c0 + n].bitcast(FP8X4), z_scale[:, c0 : c0 + n], z_bf[:].rearrange("p n t -> p (n t)")
            )

        def second_product(c0, n, ways):
            per_bank = PACK // len(ways)
            for b, (bank, copy, queue) in enumerate(ways):
                acc = psum.tile([P, per_bank * n], F32, name="acc", tag=bank)
                res = keep.tile([P, per_bank, n], F32, name=f"res{c0}_{b}", align_bytes=64)
                for k in range(per_bank):
                    a = b * per_bank + k
                    nc.tensor.matmul_mx(
                        acc[:, k * n : (k + 1) * n],
                        lhsT=w2_codes[:, a * P : (a + 1) * P].bitcast(FP8X4),
                        lhsT_scale=w2_scale[:, a * P : (a + 1) * P],
                        rhs=z_codes[:, c0 : c0 + n].bitcast(FP8X4),
                        rhs_scale=z_scale[:, c0 : c0 + n],
                        start=True,
                        stop=True,
                    )
                copy(res[:].rearrange("p a c -> p (a c)"), acc[:])
                queue.dma_start(out_rows[:, b * per_bank : (b + 1) * per_bank, c0 : c0 + n], res[:])

        last = HALF + QUARTER
        z_a = keep.tile([P, HALF, PACK], BF16, name="z_a", align_bytes=64)
        z_b = keep.tile([P, QUARTER, PACK], BF16, name="z_b", align_bytes=64)
        z_c = keep.tile([P, QUARTER, PACK], BF16, name="z_c", align_bytes=64)

        def last_pair(u, tag, copy):
            sums_c = keep.tile([P, 2, QUARTER], F32, name="sums_c", tag=tag, align_bytes=64)
            for k in range(2):
                t = 2 * u + k
                add_second(t, last, QUARTER, part_right[t][:, QUARTER:HALF], sums_c[:, k, :])
            interleave(copy, z_c[:, :, 2 * u : 2 * u + 2], sums_c[:])

        interleave(nc.scalar.copy, z_a[:], sums_a[:])
        quantise_z(0, HALF, z_a)
        interleave(nc.scalar.copy, z_b[:], sums_b[:])
        quantise_z(HALF, QUARTER, z_b)
        last_pair(0, "sums_a", nc.scalar.copy)
        second_product(0, HALF, (("bank5", nc.scalar.copy, nc.sync), ("bank6", nc.scalar.copy, nc.sync)))
        second_product(HALF, QUARTER, (("bank7", nc.scalar.copy, nc.sync),))
        last_pair(1, "base3", nc.vector.tensor_copy)
        quantise_z(last, QUARTER, z_c)
        second_product(last, QUARTER, (("bank0", nc.vector.tensor_copy, nc.sync), ("bank1", nc.scalar.copy, nc.scalar)))
